import numpy as np
import ml_dtypes


def mxq(x, axis, fmt="e4m3"):
    dtype, down = {"e4m3": (ml_dtypes.float8_e4m3fn, 7), "e5m2": (ml_dtypes.float8_e5m2, 14)}[fmt]
    v = np.moveaxis(np.asarray(x, np.float32).astype(ml_dtypes.bfloat16).astype(np.float64), axis, -1)
    blocks = v.reshape(v.shape[:-1] + (-1, 32))
    amax = np.abs(blocks).max(-1, keepdims=True)
    byte = np.maximum(np.where(amax > 0, np.frexp(amax)[1] - 1 + 127, 0) - down, 1)
    scale = np.exp2(byte - 127.0)
    codes = (blocks / scale).astype(np.float32).astype(dtype).astype(np.float64)
    return np.moveaxis((codes * scale).reshape(v.shape), -1, axis)


WIDE = False


def mx_kscale(k):
    if not WIDE:
        return np.ones(k)
    levels = np.array([10, -10, 5, -5, 0])
    if k % 512:
        return np.exp2(np.random.permutation(np.resize(levels, k // 32))).repeat(32)
    a = np.empty((k // 512, 16))
    for p in range(k // 512):
        a[p, :8] = np.random.permutation(np.resize(levels, 8))
        for g in range(8):
            far = levels[np.abs(levels - a[p, g]) >= 10]
            a[p, g + 8] = far[np.random.randint(len(far))]
    return np.exp2(a.ravel()).repeat(32)


def f64(x):
    return np.asarray(x).astype(np.float64)


def striped8(idx):
    return np.asarray(idx).reshape(8, -1, 16).transpose(0, 2, 1).reshape(128, -1).astype(np.uint16)


def unstriped8(offs):
    return offs.reshape(8, 16, -1).transpose(0, 2, 1).reshape(8, -1).astype(np.int64)


def pick8(x, idx, run):
    r = np.arange(len(x))
    return x[r[:, None], idx[r % (8 * run) // run]]


E2M1 = np.array([0.0, 0.5, 1.0, 1.5, 2.0, 3.0, 4.0, 6.0, -0.0, -0.5, -1.0, -1.5, -2.0, -3.0, -4.0, -6.0])


def pack_weight(w, fmt):
    k, n = w.shape
    w = f64(np.asarray(w, np.float32).astype(ml_dtypes.bfloat16)).reshape(k // 32, 32, n)
    amax = np.abs(w).max(1)
    if fmt == "e4m3":
        byte = np.frexp(amax)[1] - 1 + 127 - 7
    else:
        mant, ex = np.frexp(amax / 6.0)
        byte = np.where(mant > 0.5, ex, ex - 1) + 127
    byte = np.clip(np.where(amax > 0, byte, 1), 1, 254)
    scaled = (w * np.exp2(127.0 - byte)[:, None, :]).reshape(k, n).astype(np.float32)
    by_word = np.ascontiguousarray(scaled.reshape(k // 512, 128, 4, n).transpose(0, 1, 3, 2))
    if fmt == "e4m3":
        words = by_word.astype(ml_dtypes.float8_e4m3fn).view(np.uint8)
    else:
        c = by_word.astype(ml_dtypes.float4_e2m1fn).view(np.uint8) & 0xF
        words = (c[..., 0::2] | (c[..., 1::2] << 4)).reshape(k // 512, 128, 2 * n)
    return np.ascontiguousarray(words), np.ascontiguousarray(byte.astype(np.uint8).reshape(k // 512, 16, n))


def unpack_weight(words, scales, fmt):
    g, _, n = scales.shape
    words = np.ascontiguousarray(words).reshape(g, 128, n, -1)
    if fmt == "e4m3":
        vals = words.view(ml_dtypes.float8_e4m3fn).astype(np.float64)
    else:
        nib = np.empty((g, 128, n, 4), np.uint8)
        nib[..., 0::2] = words & 0xF
        nib[..., 1::2] = words >> 4
        vals = E2M1[nib]
    vals = vals * np.repeat(np.exp2(scales.astype(np.float64) - 127.0), 8, axis=1)[..., None]
    return vals.transpose(0, 1, 3, 2).reshape(g * 512, n)


D, T, U, I, J, Q = 512, 1024, 1024, 512, 256, 128


def setup_inputs():
    n = np.random.standard_normal
    idx = np.stack([np.random.permutation(T)[:I] for _ in range(8)])
    idx2 = np.stack([np.random.permutation(U)[:I] for _ in range(8)])
    idx3 = np.stack([np.random.permutation(U)[:J] for _ in range(8)])
    idx4 = np.stack([np.random.permutation(U)[:I] for _ in range(8)])
    fd = mx_kscale(D)
    keysp = pack_weight(n((D, T)) / fd[:, None], "e2m1")
    notesp = pack_weight(n((D, U)) / fd[:, None], "e4m3")
    return {
        "query": (n((D, Q)) * 1.0 / np.sqrt(D) * fd[:, None]).astype(np.float32),
        "keys_words": keysp[0],
        "keys_scales": keysp[1],
        "notes_words": notesp[0],
        "notes_scales": notesp[1],
        "offs": striped8(idx),
        "offs2": striped8(idx2),
        "offs3": striped8(idx3),
        "offs4": striped8(idx4),
    }


def reference(query, keys_words, keys_scales, notes_words, notes_scales, offs, offs2, offs3, offs4):
    idx = unstriped8(offs)
    idx2 = unstriped8(offs2)
    idx3 = unstriped8(offs3)
    idx4 = unstriped8(offs4)
    keysu = unpack_weight(keys_words, keys_scales, "e2m1")
    notesu = unpack_weight(notes_words, notes_scales, "e4m3")
    queryq = mxq(f64(query), 0, "e4m3")
    a = queryq.T @ keysu
    b = queryq.T @ notesu
    w = pick8(a, idx, 16) + pick8(b, idx2, 16)
    m2 = w.reshape(Q, J, I // J).max(axis=2)
    f1 = np.zeros((Q, U))
    f1[np.arange(Q)[:, None], idx3[np.arange(Q) % 128 // 16]] = m2
    cc = b + f1
    y = pick8(cc, idx4, 16) - w
    return y

@@ -1,0 +1,141 @@
+from contextlib import ExitStack
+
+import concourse.mybir as mybir
+
+D, T, U, I, J, Q = 512, 1024, 1024, 512, 256, 128
+FLOPS = 2 * D * Q * (T + U)
+
+F32 = mybir.dt.float32
+BF16 = mybir.dt.bfloat16
+I32 = mybir.dt.int32
+U32 = mybir.dt.uint32
+U16 = mybir.dt.uint16
+U8 = mybir.dt.uint8
+FP8X4 = mybir.dt.float8_e4m3fn_x4
+FP4X4 = mybir.dt.float4_e2m1fn_x4
+ADD = mybir.AluOpType.add
+SUB = mybir.AluOpType.subtract
+MAX = mybir.AluOpType.max
+COPY = mybir.ActivationFunctionType.Copy
+
+P = 128
+HALF = I // 2
+
+
+def load_scale_rows(queues, plane, scales):
+    for quad, queue in enumerate(queues):
+        queue.dma_start(
+            out=plane[32 * quad : 32 * quad + 4, :].bitcast(I32),
+            in_=scales[0, 4 * quad : 4 * quad + 4, :].bitcast(I32),
+        )
+
+
+def tile_attend_pairwinners_two_kernel(
+    tc, query, keys_words, keys_scales, notes_words, notes_scales, offs, offs2, offs3, offs4, out
+):
+    nc = tc.nc
+    with ExitStack() as ctx:
+        sb = ctx.enter_context(tc.tile_pool(name="sb", bufs=1))
+        ps = ctx.enter_context(tc.psum_pool(name="ps", bufs=1))
+
+        key_plane = sb.tile([P, T], U8, align_bytes=64)
+        note_plane = sb.tile([P, U], U8, align_bytes=64)
+        placed = sb.tile([P, U], F32)
+        nc.vector.memset(key_plane[:].bitcast(I32), 0)
+        nc.vector.memset(note_plane[:].bitcast(I32), 0)
+        nc.vector.memset(placed[:], 0.0)
+
+        q_raw = sb.tile([P, 4, Q], F32)
+        key_words = sb.tile([P, 2 * T], U8, align_bytes=64)
+        note_words = sb.tile([P, 4 * U], U8, align_bytes=64)
+        token_list = sb.tile([P, I // 16], U16)
+        note_list = sb.tile([P, I // 16], U16)
+        pair_list = sb.tile([P, J // 16], U16)
+        result_list = sb.tile([P, I // 16], U16)
+        nc.sync.dma_start(out=q_raw[:], in_=query.rearrange("(p j) q -> p j q", j=4))
+        load_scale_rows((nc.scalar, nc.sync, nc.scalar, nc.sync), key_plane, keys_scales)
+        nc.sync.dma_start(token_list[:], offs)
+        nc.sync.dma_start(out=key_words[:].bitcast(I32), in_=keys_words[0].bitcast(I32))
+        nc.sync.dma_start(
+            out=note_words[:].bitcast(I32),
+            in_=notes_words[0].rearrange("p n t -> p (n t)").bitcast(I32),
+        )
+        load_scale_rows((nc.gpsimd, nc.sync, nc.sync, nc.sync), note_plane, notes_scales)
+        nc.sync.dma_start(note_list[:], offs2)
+        nc.sync.dma_start(pair_list[:], offs3)
+        nc.sync.dma_start(result_list[:], offs4)
+
+        q_grouped = sb.tile([P, Q, 4], BF16, align_bytes=64)
+        q_codes = sb.tile([P, Q], U32, align_bytes=64)
+        q_plane = sb.tile([P, Q], U8, align_bytes=64)
+        for lo, hi in ((0, Q // 2), (Q // 2, Q)):
+            nc.vector.tensor_copy(
+                out=q_grouped[:, lo:hi, :].rearrange("p (c i) t -> p c t i", i=4),
+                in_=q_raw[:, :, lo:hi].rearrange("p t (c i) -> p c t i", i=4),
+            )
+        for lo, hi in ((0, Q // 2), (Q // 2, Q)):
+            nc.vector.quantize_mx(
+                out=q_codes[:, lo:hi].bitcast(FP8X4),
+                scales=q_plane[:, lo:hi],
+                in_=q_grouped[:, lo:hi, :].rearrange("p w j -> p (w j)"),
+            )
+
+        a = sb.tile([P, T], F32)
+        b = sb.tile([P, U], F32)
+        pieces = [(lo, lo + 256) for lo in range(0, 1024, 256)]
+        a_banks = [ps.tile([P, hi - lo], F32, name="a_bank%d" % lo) for lo, hi in pieces]
+        b_banks = [ps.tile([P, hi - lo], F32, name="b_bank%d" % lo) for lo, hi in pieces]
+        for bank, (lo, hi) in zip(a_banks, pieces):
+            nc.tensor.matmul_mx(
+                out=bank[:],
+                lhsT=q_codes[:].bitcast(FP8X4),
+                lhsT_scale=q_plane[:],
+                rhs=key_words[:, 2 * lo : 2 * hi].bitcast(FP4X4),
+                rhs_scale=key_plane[:, lo:hi],
+                start=True,
+                stop=True,
+            )
+        for bank, (lo, hi) in zip(b_banks, pieces):
+            nc.tensor.matmul_mx(
+                out=bank[:],
+                lhsT=q_codes[:].bitcast(FP8X4),
+                lhsT_scale=q_plane[:],
+                rhs=note_words[:, 4 * lo : 4 * hi].bitcast(FP8X4),
+                rhs_scale=note_plane[:, lo:hi],
+                start=True,
+                stop=True,
+            )
+
+        for k, (bank, (lo, hi)) in enumerate(zip(a_banks, pieces)):
+            if k % 2 == 0:
+                nc.vector.tensor_copy(out=a[:, lo:hi], in_=bank[:])
+            else:
+                nc.scalar.activation(a[:, lo:hi], bank[:], COPY)
+        for bank, (lo, hi) in zip(b_banks, pieces):
+            nc.vector.tensor_copy(out=b[:, lo:hi], in_=bank[:])
+
+        a_picked = [sb.tile([P, HALF], F32, name="a_picked%d" % h) for h in range(2)]
+        nc.scalar.activation(a_picked[0][:], a[:].indirect(token_list[:, 0:16]), COPY)
+        nc.scalar.activation(a_picked[1][:], a[:].indirect(token_list[:, 16:32]), COPY)
+        b_picked = sb.tile([P, HALF], F32)
+        nc.scalar.activation(b_picked[:], b[:].indirect(note_list[:, 16:32]), COPY)
+
+        bids = [sb.tile([P, HALF], F32, name="bids%d" % h) for h in range(2)]
+        best = [sb.tile([P, HALF // 2], F32, name="best%d" % h) for h in range(2)]
+        nc.vector.tensor_tensor(bids[0][:], b[:].indirect(note_list[:, 0:16]), a_picked[0][:], ADD)
+        nc.vector.tensor_tensor(bids[1][:], b_picked[:], a_picked[1][:], ADD)
+        nc.vector.tensor_tensor(best[0][:], bids[0][:, 0::2], bids[0][:, 1::2], MAX)
+        nc.vector.tensor_tensor(best[1][:], bids[1][:, 0::2], bids[1][:, 1::2], MAX)
+        nc.vector.tensor_copy(placed[:].indirect(pair_list[:, 0:8]), best[0][:])
+        nc.vector.tensor_copy(placed[:].indirect(pair_list[:, 8:16]), best[1][:])
+
+        cc = sb.tile([P, U], F32)
+        nc.vector.tensor_tensor(cc[:], b[:], placed[:], ADD)
+
+        result = [sb.tile([P, HALF], F32, name="result%d" % h) for h in range(2)]
+        cc_picked = sb.tile([P, HALF], F32)
+        nc.scalar.activation(cc_picked[:], cc[:].indirect(result_list[:, 16:32]), COPY)
+        nc.vector.tensor_tensor(result[0][:], cc[:].indirect(result_list[:, 0:16]), bids[0][:], SUB)
+        nc.sync.dma_start(out=out[:, 0:HALF], in_=result[0][:])
+        nc.vector.tensor_tensor(result[1][:], cc_picked[:], bids[1][:], SUB)
+        nc.sync.dma_start(out=out[:, HALF:I], in_=result[1][:])

@@ -106,31 +106,31 @@ def tile_attend_pairwinners_two_kernel(
                 stop=True,
             )
 
-        for k, (bank, (lo, hi)) in enumerate(zip(a_banks, pieces)):
-            if k % 2 == 0:
-                nc.vector.tensor_copy(out=a[:, lo:hi], in_=bank[:])
-            else:
-                nc.scalar.activation(a[:, lo:hi], bank[:], COPY)
+        for bank, (lo, hi) in zip(a_banks[:-1], pieces):
+            nc.vector.tensor_copy(out=a[:, lo:hi], in_=bank[:])
+        nc.scalar.activation(a[:, pieces[-1][0] : T], a_banks[-1][:], COPY)
         for bank, (lo, hi) in zip(b_banks, pieces):
-            nc.vector.tensor_copy(out=b[:, lo:hi], in_=bank[:])
+            nc.scalar.activation(b[:, lo:hi], bank[:], COPY)
 
         a_picked = [sb.tile([P, HALF], F32, name="a_picked%d" % h) for h in range(2)]
-        nc.scalar.activation(a_picked[0][:], a[:].indirect(token_list[:, 0:16]), COPY)
-        nc.scalar.activation(a_picked[1][:], a[:].indirect(token_list[:, 16:32]), COPY)
+        nc.vector.tensor_copy(a_picked[0][:], a[:].indirect(token_list[:, 0:16]))
+        nc.vector.tensor_copy(a_picked[1][:], a[:].indirect(token_list[:, 16:32]))
         b_picked = sb.tile([P, HALF], F32)
         nc.scalar.activation(b_picked[:], b[:].indirect(note_list[:, 16:32]), COPY)
 
         bids = [sb.tile([P, HALF], F32, name="bids%d" % h) for h in range(2)]
         best = [sb.tile([P, HALF // 2], F32, name="best%d" % h) for h in range(2)]
         nc.vector.tensor_tensor(bids[0][:], b[:].indirect(note_list[:, 0:16]), a_picked[0][:], ADD)
-        nc.vector.tensor_tensor(bids[1][:], b_picked[:], a_picked[1][:], ADD)
         nc.vector.tensor_tensor(best[0][:], bids[0][:, 0::2], bids[0][:, 1::2], MAX)
-        nc.vector.tensor_tensor(best[1][:], bids[1][:, 0::2], bids[1][:, 1::2], MAX)
+        nc.vector.tensor_tensor(bids[1][:], b_picked[:], a_picked[1][:], ADD)
         nc.vector.tensor_copy(placed[:].indirect(pair_list[:, 0:8]), best[0][:])
+        nc.vector.tensor_tensor(best[1][:], bids[1][:, 0::2], bids[1][:, 1::2], MAX)
         nc.vector.tensor_copy(placed[:].indirect(pair_list[:, 8:16]), best[1][:])
 
         cc = sb.tile([P, U], F32)
-        nc.vector.tensor_tensor(cc[:], b[:], placed[:], ADD)
+        for bank, (lo, hi) in zip(b_banks[:-1], pieces):
+            nc.vector.tensor_tensor(cc[:, lo:hi], bank[:], placed[:, lo:hi], ADD)
+        nc.gpsimd.tensor_tensor(cc[:, 768:U], b[:, 768:U], placed[:, 768:U], ADD)
 
         result = [sb.tile([P, HALF], F32, name="result%d" % h) for h in range(2)]
         cc_picked = sb.tile([P, HALF], F32)

from contextlib import ExitStack

import concourse.mybir as mybir

D, T, U, I, J, Q = 512, 1024, 1024, 512, 256, 128
FLOPS = 2 * D * Q * (T + U)

F32 = mybir.dt.float32
BF16 = mybir.dt.bfloat16
I32 = mybir.dt.int32
U32 = mybir.dt.uint32
U16 = mybir.dt.uint16
U8 = mybir.dt.uint8
FP8X4 = mybir.dt.float8_e4m3fn_x4
FP4X4 = mybir.dt.float4_e2m1fn_x4
ADD = mybir.AluOpType.add
SUB = mybir.AluOpType.subtract
MAX = mybir.AluOpType.max
COPY = mybir.ActivationFunctionType.Copy

P = 128
HALF = I // 2


def load_scale_rows(queues, plane, scales):
    for quad, queue in enumerate(queues):
        queue.dma_start(
            out=plane[32 * quad : 32 * quad + 4, :].bitcast(I32),
            in_=scales[0, 4 * quad : 4 * quad + 4, :].bitcast(I32),
        )


def tile_attend_pairwinners_two_kernel(
    tc, query, keys_words, keys_scales, notes_words, notes_scales, offs, offs2, offs3, offs4, out
):
    nc = tc.nc
    with ExitStack() as ctx:
        sb = ctx.enter_context(tc.tile_pool(name="sb", bufs=1))
        ps = ctx.enter_context(tc.psum_pool(name="ps", bufs=1))

        key_plane = sb.tile([P, T], U8, align_bytes=64)
        note_plane = sb.tile([P, U], U8, align_bytes=64)
        placed = sb.tile([P, U], F32)
        nc.vector.memset(key_plane[:].bitcast(I32), 0)
        nc.vector.memset(note_plane[:].bitcast(I32), 0)
        nc.vector.memset(placed[:], 0.0)

        q_raw = sb.tile([P, 4, Q], F32)
        key_words = sb.tile([P, 2 * T], U8, align_bytes=64)
        note_words = sb.tile([P, 4 * U], U8, align_bytes=64)
        token_list = sb.tile([P, I // 16], U16)
        note_list = sb.tile([P, I // 16], U16)
        pair_list = sb.tile([P, J // 16], U16)
        result_list = sb.tile([P, I // 16], U16)
        nc.sync.dma_start(out=q_raw[:], in_=query.rearrange("(p j) q -> p j q", j=4))
        load_scale_rows((nc.scalar, nc.sync, nc.scalar, nc.sync), key_plane, keys_scales)
        nc.sync.dma_start(token_list[:], offs)
        nc.sync.dma_start(out=key_words[:].bitcast(I32), in_=keys_words[0].bitcast(I32))
        nc.sync.dma_start(
            out=note_words[:].bitcast(I32),
            in_=notes_words[0].rearrange("p n t -> p (n t)").bitcast(I32),
        )
        load_scale_rows((nc.gpsimd, nc.sync, nc.sync, nc.sync), note_plane, notes_scales)
        nc.sync.dma_start(note_list[:], offs2)
        nc.sync.dma_start(pair_list[:], offs3)
        nc.sync.dma_start(result_list[:], offs4)

        q_grouped = sb.tile([P, Q, 4], BF16, align_bytes=64)
        q_codes = sb.tile([P, Q], U32, align_bytes=64)
        q_plane = sb.tile([P, Q], U8, align_bytes=64)
        for lo, hi in ((0, Q // 2), (Q // 2, Q)):
            nc.vector.tensor_copy(
                out=q_grouped[:, lo:hi, :].rearrange("p (c i) t -> p c t i", i=4),
                in_=q_raw[:, :, lo:hi].rearrange("p t (c i) -> p c t i", i=4),
            )
        for lo, hi in ((0, Q // 2), (Q // 2, Q)):
            nc.vector.quantize_mx(
                out=q_codes[:, lo:hi].bitcast(FP8X4),
                scales=q_plane[:, lo:hi],
                in_=q_grouped[:, lo:hi, :].rearrange("p w j -> p (w j)"),
            )

        a = sb.tile([P, T], F32)
        b = sb.tile([P, U], F32)
        pieces = [(lo, lo + 256) for lo in range(0, 1024, 256)]
        a_banks = [ps.tile([P, hi - lo], F32, name="a_bank%d" % lo) for lo, hi in pieces]
        b_banks = [ps.tile([P, hi - lo], F32, name="b_bank%d" % lo) for lo, hi in pieces]
        for bank, (lo, hi) in zip(a_banks, pieces):
            nc.tensor.matmul_mx(
                out=bank[:],
                lhsT=q_codes[:].bitcast(FP8X4),
                lhsT_scale=q_plane[:],
                rhs=key_words[:, 2 * lo : 2 * hi].bitcast(FP4X4),
                rhs_scale=key_plane[:, lo:hi],
                start=True,
                stop=True,
            )
        for bank, (lo, hi) in zip(b_banks, pieces):
            nc.tensor.matmul_mx(
                out=bank[:],
                lhsT=q_codes[:].bitcast(FP8X4),
                lhsT_scale=q_plane[:],
                rhs=note_words[:, 4 * lo : 4 * hi].bitcast(FP8X4),
                rhs_scale=note_plane[:, lo:hi],
                start=True,
                stop=True,
            )

        for bank, (lo, hi) in zip(a_banks[:-1], pieces):
            nc.vector.tensor_copy(out=a[:, lo:hi], in_=bank[:])
        nc.scalar.activation(a[:, pieces[-1][0] : T], a_banks[-1][:], COPY)
        for bank, (lo, hi) in zip(b_banks, pieces):
            nc.scalar.activation(b[:, lo:hi], bank[:], COPY)

        a_picked = [sb.tile([P, HALF], F32, name="a_picked%d" % h) for h in range(2)]
        nc.vector.tensor_copy(a_picked[0][:], a[:].indirect(token_list[:, 0:16]))
        nc.vector.tensor_copy(a_picked[1][:], a[:].indirect(token_list[:, 16:32]))
        b_picked = sb.tile([P, HALF], F32)
        nc.scalar.activation(b_picked[:], b[:].indirect(note_list[:, 16:32]), COPY)

        bids = [sb.tile([P, HALF], F32, name="bids%d" % h) for h in range(2)]
        best = [sb.tile([P, HALF // 2], F32, name="best%d" % h) for h in range(2)]
        nc.vector.tensor_tensor(bids[0][:], b[:].indirect(note_list[:, 0:16]), a_picked[0][:], ADD)
        nc.vector.tensor_tensor(best[0][:], bids[0][:, 0::2], bids[0][:, 1::2], MAX)
        nc.vector.tensor_tensor(bids[1][:], b_picked[:], a_picked[1][:], ADD)
        nc.vector.tensor_copy(placed[:].indirect(pair_list[:, 0:8]), best[0][:])
        nc.vector.tensor_tensor(best[1][:], bids[1][:, 0::2], bids[1][:, 1::2], MAX)
        nc.vector.tensor_copy(placed[:].indirect(pair_list[:, 8:16]), best[1][:])

        cc = sb.tile([P, U], F32)
        for bank, (lo, hi) in zip(b_banks[:-1], pieces):
            nc.vector.tensor_tensor(cc[:, lo:hi], bank[:], placed[:, lo:hi], ADD)
        nc.gpsimd.tensor_tensor(cc[:, 768:U], b[:, 768:U], placed[:, 768:U], ADD)

        result = [sb.tile([P, HALF], F32, name="result%d" % h) for h in range(2)]
        cc_picked = sb.tile([P, HALF], F32)
        nc.scalar.activation(cc_picked[:], cc[:].indirect(result_list[:, 16:32]), COPY)
        nc.vector.tensor_tensor(result[0][:], cc[:].indirect(result_list[:, 0:16]), bids[0][:], SUB)
        nc.sync.dma_start(out=out[:, 0:HALF], in_=result[0][:])
        nc.vector.tensor_tensor(result[1][:], cc_picked[:], bids[1][:], SUB)
        nc.sync.dma_start(out=out[:, HALF:I], in_=result[1][:])
